import numpy as np
import ml_dtypes


def mxq(x, axis, fmt="e4m3"):
    dtype, down = {"e4m3": (ml_dtypes.float8_e4m3fn, 7), "e5m2": (ml_dtypes.float8_e5m2, 14)}[fmt]
    v = np.moveaxis(np.asarray(x, np.float32).astype(ml_dtypes.bfloat16).astype(np.float64), axis, -1)
    blocks = v.reshape(v.shape[:-1] + (-1, 32))
    amax = np.abs(blocks).max(-1, keepdims=True)
    byte = np.maximum(np.where(amax > 0, np.frexp(amax)[1] - 1 + 127, 0) - down, 1)
    scale = np.exp2(byte - 127.0)
    codes = (blocks / scale).astype(np.float32).astype(dtype).astype(np.float64)
    return np.moveaxis((codes * scale).reshape(v.shape), -1, axis)


WIDE = False


def mx_kscale(k):
    if not WIDE:
        return np.ones(k)
    levels = np.array([10, -10, 5, -5, 0])
    if k % 512:
        return np.exp2(np.random.permutation(np.resize(levels, k // 32))).repeat(32)
    a = np.empty((k // 512, 16))
    for p in range(k // 512):
        a[p, :8] = np.random.permutation(np.resize(levels, 8))
        for g in range(8):
            far = levels[np.abs(levels - a[p, g]) >= 10]
            a[p, g + 8] = far[np.random.randint(len(far))]
    return np.exp2(a.ravel()).repeat(32)


def f64(x):
    return np.asarray(x).astype(np.float64)


def striped(idx):
    return np.tile(idx.reshape(-1, 16).T, (8, 1)).astype(np.uint16)


def unstriped(offs):
    return offs[:16].T.reshape(-1).astype(np.int64)


E2M1 = np.array([0.0, 0.5, 1.0, 1.5, 2.0, 3.0, 4.0, 6.0, -0.0, -0.5, -1.0, -1.5, -2.0, -3.0, -4.0, -6.0])


def pack_weight(w, fmt):
    k, n = w.shape
    w = f64(np.asarray(w, np.float32).astype(ml_dtypes.bfloat16)).reshape(k // 32, 32, n)
    amax = np.abs(w).max(1)
    if fmt == "e4m3":
        byte = np.frexp(amax)[1] - 1 + 127 - 7
    else:
        mant, ex = np.frexp(amax / 6.0)
        byte = np.where(mant > 0.5, ex, ex - 1) + 127
    byte = np.clip(np.where(amax > 0, byte, 1), 1, 254)
    scaled = (w * np.exp2(127.0 - byte)[:, None, :]).reshape(k, n).astype(np.float32)
    by_word = np.ascontiguousarray(scaled.reshape(k // 512, 128, 4, n).transpose(0, 1, 3, 2))
    if fmt == "e4m3":
        words = by_word.astype(ml_dtypes.float8_e4m3fn).view(np.uint8)
    else:
        c = by_word.astype(ml_dtypes.float4_e2m1fn).view(np.uint8) & 0xF
        words = (c[..., 0::2] | (c[..., 1::2] << 4)).reshape(k // 512, 128, 2 * n)
    return np.ascontiguousarray(words), np.ascontiguousarray(byte.astype(np.uint8).reshape(k // 512, 16, n))


def unpack_weight(words, scales, fmt):
    g, _, n = scales.shape
    words = np.ascontiguousarray(words).reshape(g, 128, n, -1)
    if fmt == "e4m3":
        vals = words.view(ml_dtypes.float8_e4m3fn).astype(np.float64)
    else:
        nib = np.empty((g, 128, n, 4), np.uint8)
        nib[..., 0::2] = words & 0xF
        nib[..., 1::2] = words >> 4
        vals = E2M1[nib]
    vals = vals * np.repeat(np.exp2(scales.astype(np.float64) - 127.0), 8, axis=1)[..., None]
    return vals.transpose(0, 1, 3, 2).reshape(g * 512, n)


def gelu(v):
    return 0.5 * v * (1.0 + np.tanh(np.sqrt(2.0 / np.pi) * (v + 0.044715 * v**3)))


K, H, T, S, T2, P = 1024, 512, 2048, 1024, 2048, 512

def setup_inputs():
    n = np.random.standard_normal
    s, u = mx_kscale(K)[:, None], mx_kscale(H)[:, None]
    tab_words, tab_scales = pack_weight(n((K, T)) * s, "e4m3")
    w1 = n((K, H)) / np.sqrt(K) / s * u.T
    w2_words, w2_scales = pack_weight(1.4 * n((K, H)) / np.sqrt(K) / s, "e2m1")
    w3_words, w3_scales = pack_weight(0.8 * n((K, H)) / np.sqrt(K) / s * u.T, "e4m3")
    perm = np.random.permutation(T2)
    return {"tab_words": tab_words, "tab_scales": tab_scales,
            "offs": striped(np.random.permutation(T)[:S]),
            "w1": w1.astype(np.float32),
            "w2_words": w2_words, "w2_scales": w2_scales,
            "w3_words": w3_words, "w3_scales": w3_scales,
            "page0": (n((H, T2)) * u).astype(np.float32),
            "wgs": np.exp(0.3 * n((128, S))).astype(np.float32),
            "offs2": striped(np.random.permutation(T2)[:S]),
            "offs3": striped(perm[:P]),
            "offs4": striped(perm[P:2 * P]),
            "w4": (n((H, H)) / np.sqrt(H) / u).astype(np.float32),
            "skip": (np.exp(0.3 * n(H)) / u[:, 0]).astype(np.float32)}

def reference(tab_words, tab_scales, offs, w1, w2_words, w2_scales, w3_words, w3_scales,
              page0, wgs, offs2, offs3, offs4, w4, skip):
    v = unpack_weight(tab_words, tab_scales, "e4m3")[:, unstriped(offs)]
    w2 = unpack_weight(w2_words, w2_scales, "e2m1")
    w3 = unpack_weight(w3_words, w3_scales, "e4m3")
    lead = mxq(f64(w1), 0, "e4m3").T @ v
    bend = np.tanh(w2.T @ v)
    h = lead * bend + (w3.T @ v)
    page = f64(page0).copy()
    page[:, unstriped(offs2)] = np.tile(f64(wgs), (H // 128, 1)) * h
    a = page[:, unstriped(offs3)]
    b = page[:, unstriped(offs4)]
    page[:, unstriped(offs3)] = np.maximum(a, b)
    page[:, unstriped(offs4)] = np.minimum(a, b)
    y = mxq(f64(w4), 0, "e4m3").T @ mxq(page, 0, "e4m3")
    return y + f64(skip)[:, None] * page

@@ -1,0 +1,237 @@
+from contextlib import ExitStack
+
+import concourse.mybir as mybir
+from concourse.masks import make_identity
+
+K, H, T, S, T2, PAIRS = 1024, 512, 2048, 1024, 2048, 512
+FLOPS = 2 * (3 * K * H * S + H * H * T2)
+
+F32 = mybir.dt.float32
+BF16 = mybir.dt.bfloat16
+I32 = mybir.dt.int32
+U32 = mybir.dt.uint32
+U16 = mybir.dt.uint16
+U8 = mybir.dt.uint8
+E4M3 = mybir.dt.float8_e4m3fn_x4
+E2M1 = mybir.dt.float4_e2m1fn_x4
+ALU = mybir.AluOpType
+ACT = mybir.ActivationFunctionType
+
+P = 128
+PACK = 4
+PASSES = K // (P * PACK)
+BANK = 512
+HALVES = S // BANK
+BLOCKS = BANK // P
+SPANS = T2 // BANK
+
+
+def tile_list_leave_ledger_exchange_kernel(
+    tc, tab_words, tab_scales, offs, w1, w2_words, w2_scales, w3_words, w3_scales,
+    page0, wgs, offs2, offs3, offs4, w4, skip, out,
+):
+    nc = tc.nc
+    with ExitStack() as ctx:
+        keep = ctx.enter_context(tc.tile_pool(name="keep", bufs=1))
+        ring = ctx.enter_context(tc.tile_pool(name="ring", bufs=2))
+        psum = ctx.enter_context(tc.psum_pool(name="psum", bufs=1))
+
+        def held(shape, dtype, name):
+            return keep.tile(shape, dtype, name=name, align_bytes=64)
+
+        def staged(name):
+            return ring.tile([P, BANK], F32, name=name, tag="staged", bufs=16)
+
+        def load_list(src, name):
+            tile = keep.tile([P, src.shape[1]], U16, name=name)
+            nc.sync.dma_start(tile[:], src)
+            return tile
+
+        def load_scales(queue, zeroer, src, name):
+            tile = held([P, PASSES, src.shape[2]], U8, name)
+            zeroer.memset(tile[:].bitcast(I32), 0)
+            for q in range(4):
+                queue.dma_start(
+                    out=tile[32 * q : 32 * q + 4, :, :].bitcast(I32),
+                    in_=src[:, 4 * q : 4 * q + 4, :].rearrange("a r n -> r a n").bitcast(I32),
+                )
+            return tile
+
+        pick = load_list(offs, "pick")
+        tab_s = load_scales(nc.scalar, nc.vector, tab_scales, "tab_s")
+        w2_s = load_scales(nc.scalar, nc.gpsimd, w2_scales, "w2_s")
+        w3_s = load_scales(nc.scalar, nc.gpsimd, w3_scales, "w3_s")
+        tab_w = []
+        for a in range(PASSES):
+            tile = held([P, T], I32, "tab_w%d" % a)
+            nc.sync.dma_start(out=tile[:], in_=tab_words[a].rearrange("p t i -> p (t i)").bitcast(I32))
+            tab_w.append(tile)
+        w2_w = held([P, PASSES, 2 * H], U8, "w2_w")
+        nc.sync.dma_start(out=w2_w[:].bitcast(I32), in_=w2_words.rearrange("a p n -> p a n").bitcast(I32))
+        w3_w = held([P, PASSES, H], I32, "w3_w")
+        nc.sync.dma_start(out=w3_w[:], in_=w3_words.rearrange("a p n i -> p a (n i)").bitcast(I32))
+        w1_raw = []
+        for a in range(PASSES):
+            tile = ring.tile([P, PACK, H], F32, name="w1_raw%d" % a, tag="raw")
+            nc.sync.dma_start(out=tile[:], in_=w1[a * 512 : (a + 1) * 512, :].rearrange("(p i) n -> p i n", i=PACK))
+            w1_raw.append(tile)
+        put = load_list(offs2, "put")
+        wgs_rows = wgs.rearrange("(m t) j -> m t j", t=PACK)
+        gain_first = held([P, 1, S], F32, "gain_first")
+        gain_rest = held([P, PACK - 1, S], F32, "gain_rest")
+        page_rows = page0.rearrange("(p t) c -> p t c", t=PACK)
+        page = [held([P, T2], F32, "page%d" % t) for t in range(PACK)]
+        for q in range(4):
+            nc.sync.dma_start(out=gain_first[32 * q : 32 * q + 32, :, :], in_=wgs_rows[:, 0:1, :])
+        nc.sync.dma_start(out=page[0][:], in_=page_rows[:, 0, :])
+        for q in range(4):
+            nc.sync.dma_start(out=gain_rest[32 * q : 32 * q + 32, :, :], in_=wgs_rows[:, 1:PACK, :])
+        for t in range(1, PACK):
+            nc.sync.dma_start(out=page[t][:], in_=page_rows[:, t, :])
+        larger = load_list(offs3, "larger")
+        smaller = load_list(offs4, "smaller")
+        gain = [gain_first[:, 0, :]] + [gain_rest[:, t, :] for t in range(PACK - 1)]
+
+        ident = held([P, P], F32, "ident")
+        make_identity(nc, ident[:])
+
+        v_w = {}
+        v_s = {}
+        for u in range(HALVES):
+            entries = pick[:, u * 32 : (u + 1) * 32]
+            for a in range(PASSES):
+                v_s[a, u] = held([P, BANK], U8, "v_s%d%d" % (a, u))
+                nc.vector.tensor_copy(v_s[a, u][:], tab_s[:, a, :].indirect(entries))
+            for a in range(PASSES):
+                v_w[a, u] = held([P, BANK], U32, "v_w%d%d" % (a, u))
+                nc.vector.tensor_copy(v_w[a, u][:], tab_w[a][:].bitcast(U32).indirect(entries))
+
+        def product(u, b, codes, scales):
+            bank = psum.tile([P, BANK], F32, name="bank", tag="mx", bufs=6)
+            cols = slice(b * P, (b + 1) * P)
+            for a in range(PASSES):
+                nc.tensor.matmul_mx(
+                    out=bank[:],
+                    lhsT=v_w[a, u][:, cols].bitcast(E4M3),
+                    lhsT_scale=v_s[a, u][:, cols],
+                    rhs=codes[a],
+                    rhs_scale=scales[a],
+                    start=(a == 0),
+                    stop=(a == PASSES - 1),
+                )
+            return bank[:].rearrange("j (m t) -> j t m", t=PACK)
+
+        def by_tile(tile):
+            return tile[:].rearrange("j (t m) -> j t m", t=PACK)
+
+        bent = {}
+        third = {}
+        for u in range(HALVES):
+            for b in range(BLOCKS):
+                bent[u, b] = staged("bent")
+                third[u, b] = staged("third")
+                sums = product(u, b, [w2_w[:, a, :].bitcast(E2M1) for a in range(PASSES)], [w2_s[:, a, :] for a in range(PASSES)])
+                nc.scalar.activation(by_tile(bent[u, b]), sums, ACT.Tanh)
+                sums = product(u, b, [w3_w[:, a, :].bitcast(E4M3) for a in range(PASSES)], [w3_s[:, a, :] for a in range(PASSES)])
+                nc.scalar.copy(by_tile(third[u, b]), sums)
+
+        w1_c = []
+        w1_s = []
+        for a in range(PASSES):
+            woven = ring.tile([P, H, PACK], BF16, name="woven", tag="woven", align_bytes=64)
+            dst = woven[:].rearrange("p (c e) i -> p c i e", e=4)
+            src = w1_raw[a][:].rearrange("p i (c e) -> p c i e", e=4)
+            if a == 0:
+                nc.scalar.copy(dst, src)
+            else:
+                nc.vector.tensor_copy(dst, src)
+            w1_c.append(held([P, H], U32, "w1_c%d" % a))
+            w1_s.append(held([P, H], U8, "w1_s%d" % a))
+            nc.vector.quantize_mx(out=w1_c[a][:].bitcast(E4M3), scales=w1_s[a][:], in_=woven[:].rearrange("p n i -> p (n i)"))
+
+        fresh = [held([P, S], F32, "fresh%d" % t) for t in range(PACK)]
+
+        def turn(t, u):
+            bank = psum.tile([P, BANK], F32, name="turned", tag="turned", bufs=2)
+            rows = slice(t * P, (t + 1) * P)
+            for b in range(BLOCKS):
+                cols = slice(b * P, (b + 1) * P)
+                nc.tensor.matmul(bank[:, cols], lhsT=bent[u, b][:, rows], rhs=ident[:], is_transpose=True, start=True, stop=False)
+                nc.tensor.matmul(bank[:, cols], lhsT=third[u, b][:, rows], rhs=ident[:], is_transpose=True, start=False, stop=True)
+            nc.scalar.copy(fresh[t][:, u * BANK : (u + 1) * BANK], bank[:])
+
+        for u in range(HALVES):
+            for b in range(BLOCKS):
+                sums = product(u, b, [w1_c[a][:].bitcast(E4M3) for a in range(PASSES)], [w1_s[a][:] for a in range(PASSES)])
+                nc.vector.tensor_tensor(by_tile(bent[u, b]), sums, by_tile(bent[u, b]), ALU.mult)
+            turn(0, u)
+        for t in range(1, PACK):
+            for u in range(HALVES):
+                turn(t, u)
+
+        def replace(t, first, last):
+            nc.vector.tensor_tensor(
+                page[t][:].indirect(put[:, first // 16 : last // 16]),
+                fresh[t][:, first:last],
+                gain[t][:, first:last],
+                ALU.mult,
+            )
+
+        w4_raw = ring.tile([P, PACK, H], F32, name="w4_raw", tag="raw")
+        nc.sync.dma_start(out=w4_raw[:], in_=w4.rearrange("(p i) n -> p i n", i=PACK))
+        skip_t = held([P, PACK], F32, "skip_t")
+        nc.sync.dma_start(out=skip_t[:], in_=skip.rearrange("(p t) -> p t", t=PACK))
+        w4_woven = ring.tile([P, H, PACK], BF16, name="w4_woven", tag="woven", align_bytes=64)
+        nc.scalar.copy(
+            w4_woven[:].rearrange("p (t m) i -> p t m i", t=PACK),
+            w4_raw[:].rearrange("p i (m t) -> p t m i", t=PACK),
+        )
+        w4_c = held([P, H], U32, "w4_c")
+        w4_s = held([P, H], U8, "w4_s")
+
+        rounded = [held([P, BANK, PACK], BF16, "rounded%d" % c) for c in range(SPANS)]
+
+        for u in range(HALVES):
+            replace(0, u * BANK, (u + 1) * BANK)
+        for t in range(1, PACK):
+            replace(t, 0, S)
+        for t in range(PACK):
+            kept = ring.tile([P, PAIRS], F32, name="kept")
+            swapped = ring.tile([P, PAIRS], F32, name="swapped")
+            high = ring.tile([P, PAIRS], F32, name="high")
+            low = ring.tile([P, PAIRS], F32, name="low")
+            nc.vector.tensor_copy(kept[:], page[t][:].indirect(larger[:]))
+            nc.vector.tensor_copy(swapped[:], page[t][:].indirect(smaller[:]))
+            if t + 1 == PACK:
+                nc.vector.quantize_mx(out=w4_c[:].bitcast(E4M3), scales=w4_s[:], in_=w4_woven[:].rearrange("p n i -> p (n i)"))
+            nc.vector.tensor_tensor(high[:], kept[:], swapped[:], ALU.max)
+            nc.vector.tensor_tensor(low[:], kept[:], swapped[:], ALU.min)
+            nc.vector.tensor_copy(page[t][:].indirect(larger[:]), high[:])
+            nc.vector.tensor_copy(page[t][:].indirect(smaller[:]), low[:])
+            for c in range(SPANS):
+                nc.scalar.copy(rounded[c][:, :, t], page[t][:, c * BANK : (c + 1) * BANK])
+
+        out_rows = out.rearrange("(p t) c -> p t c", t=PACK)
+        b_c = {}
+        b_s = {}
+
+        def quantise(c):
+            b_c[c] = held([P, BANK], U32, "b_c%d" % c)
+            b_s[c] = held([P, BANK], U8, "b_s%d" % c)
+            nc.vector.quantize_mx(out=b_c[c][:].bitcast(E4M3), scales=b_s[c][:], in_=rounded[c][:].rearrange("p n i -> p (n i)"))
+
+        quantise(0)
+        for c in range(SPANS):
+            cols = slice(c * BANK, (c + 1) * BANK)
+            if c + 1 < SPANS:
+                quantise(c + 1)
+            for t in range(PACK):
+                rows = slice(t * P, (t + 1) * P)
+                bank = psum.tile([P, BANK], F32, name="bank", tag="mx", bufs=6)
+                nc.tensor.matmul_mx(
+                    out=bank[:], lhsT=w4_c[:, rows].bitcast(E4M3), lhsT_scale=w4_s[:, rows],
+                    rhs=b_c[c][:].bitcast(E4M3), rhs_scale=b_s[c][:], start=True, stop=True,
+                )
+                result = staged("result")
+                nc.vector.scalar_tensor_tensor(result[:], page[t][:, cols], skip_t[:, t : t + 1], bank[:], ALU.mult, ALU.add)
+                nc.sync.dma_start(out=out_rows[:, t, cols], in_=result[:])

@@ -23,7 +23,7 @@ PASSES = K // (P * PACK)
 BANK = 512
 HALVES = S // BANK
 BLOCKS = BANK // P
-SPANS = T2 // BANK
+SPANS = [(0, 256), (256, 512), (512, 1024), (1024, 1536), (1536, 2048)]
 
 
 def tile_list_leave_ledger_exchange_kernel(
@@ -39,8 +39,8 @@ def tile_list_leave_ledger_exchange_kernel(
         def held(shape, dtype, name):
             return keep.tile(shape, dtype, name=name, align_bytes=64)
 
-        def staged(name):
-            return ring.tile([P, BANK], F32, name=name, tag="staged", bufs=16)
+        def staged(name, width):
+            return ring.tile([P, width], F32, name=name, tag="staged", bufs=16)
 
         def load_list(src, name):
             tile = keep.tile([P, src.shape[1]], U16, name=name)
@@ -57,19 +57,23 @@ def tile_list_leave_ledger_exchange_kernel(
                 )
             return tile
 
-        pick = load_list(offs, "pick")
-        tab_s = load_scales(nc.scalar, nc.vector, tab_scales, "tab_s")
-        w2_s = load_scales(nc.scalar, nc.gpsimd, w2_scales, "w2_s")
-        w3_s = load_scales(nc.scalar, nc.gpsimd, w3_scales, "w3_s")
-        tab_w = []
-        for a in range(PASSES):
+        def load_words(a):
             tile = held([P, T], I32, "tab_w%d" % a)
             nc.sync.dma_start(out=tile[:], in_=tab_words[a].rearrange("p t i -> p (t i)").bitcast(I32))
-            tab_w.append(tile)
+            return tile
+
+        ident = held([P, P], F32, "ident")
+        make_identity(nc, ident[:])
+
+        pick = load_list(offs, "pick")
+        tab_w = [load_words(a) for a in range(PASSES)]
+        tab_s = load_scales(nc.sync, nc.vector, tab_scales, "tab_s")
         w2_w = held([P, PASSES, 2 * H], U8, "w2_w")
         nc.sync.dma_start(out=w2_w[:].bitcast(I32), in_=w2_words.rearrange("a p n -> p a n").bitcast(I32))
+        w2_s = load_scales(nc.sync, nc.gpsimd, w2_scales, "w2_s")
         w3_w = held([P, PASSES, H], I32, "w3_w")
         nc.sync.dma_start(out=w3_w[:], in_=w3_words.rearrange("a p n i -> p a (n i)").bitcast(I32))
+        w3_s = load_scales(nc.sync, nc.gpsimd, w3_scales, "w3_s")
         w1_raw = []
         for a in range(PASSES):
             tile = ring.tile([P, PACK, H], F32, name="w1_raw%d" % a, tag="raw")
@@ -77,105 +81,111 @@ def tile_list_leave_ledger_exchange_kernel(
             w1_raw.append(tile)
         put = load_list(offs2, "put")
         wgs_rows = wgs.rearrange("(m t) j -> m t j", t=PACK)
-        gain_first = held([P, 1, S], F32, "gain_first")
-        gain_rest = held([P, PACK - 1, S], F32, "gain_rest")
         page_rows = page0.rearrange("(p t) c -> p t c", t=PACK)
         page = [held([P, T2], F32, "page%d" % t) for t in range(PACK)]
-        for q in range(4):
-            nc.sync.dma_start(out=gain_first[32 * q : 32 * q + 32, :, :], in_=wgs_rows[:, 0:1, :])
-        nc.sync.dma_start(out=page[0][:], in_=page_rows[:, 0, :])
-        for q in range(4):
-            nc.sync.dma_start(out=gain_rest[32 * q : 32 * q + 32, :, :], in_=wgs_rows[:, 1:PACK, :])
-        for t in range(1, PACK):
+        gain = {}
+
+        def load_gain(first, last, u):
+            tile = keep.tile([P, last - first, BANK], F32, name="gain", tag="gain%d%d" % (first, u))
+            for q in range(4):
+                nc.sync.dma_start(out=tile[32 * q : 32 * q + 32, :, :], in_=wgs_rows[:, first:last, u * BANK : (u + 1) * BANK])
+            for t in range(first, last):
+                gain[t, u] = tile[:, t - first, :]
+
+        for t in range(PACK):
+            load_gain(t, t + 1, 0)
             nc.sync.dma_start(out=page[t][:], in_=page_rows[:, t, :])
+        load_gain(0, PACK, 1)
         larger = load_list(offs3, "larger")
         smaller = load_list(offs4, "smaller")
-        gain = [gain_first[:, 0, :]] + [gain_rest[:, t, :] for t in range(PACK - 1)]
-
-        ident = held([P, P], F32, "ident")
-        make_identity(nc, ident[:])
 
         v_w = {}
         v_s = {}
-        for u in range(HALVES):
-            entries = pick[:, u * 32 : (u + 1) * 32]
-            for a in range(PASSES):
-                v_s[a, u] = held([P, BANK], U8, "v_s%d%d" % (a, u))
-                nc.vector.tensor_copy(v_s[a, u][:], tab_s[:, a, :].indirect(entries))
-            for a in range(PASSES):
-                v_w[a, u] = held([P, BANK], U32, "v_w%d%d" % (a, u))
-                nc.vector.tensor_copy(v_w[a, u][:], tab_w[a][:].bitcast(U32).indirect(entries))
 
-        def product(u, b, codes, scales):
-            bank = psum.tile([P, BANK], F32, name="bank", tag="mx", bufs=6)
+        def gather_words(a, u):
+            v_w[a, u] = ring.tile([P, BANK], U32, name="v_w%d" % a, tag="v_w%d" % a, bufs=PASSES - a, align_bytes=64)
+            nc.vector.tensor_copy(v_w[a, u][:], tab_w[a][:].bitcast(U32).indirect(pick[:, u * 32 : (u + 1) * 32]))
+
+        def gather_scales(a, u):
+            v_s[a, u] = held([P, BANK], U8, "v_s%d%d" % (a, u))
+            nc.vector.tensor_copy(v_s[a, u][:], tab_s[:, a, :].indirect(pick[:, u * 32 : (u + 1) * 32]))
+
+        def mx_bank():
+            return psum.tile([P, BANK], F32, name="bank", tag="mx", bufs=6)
+
+        def one_pass(bank, u, b, a, codes, scales):
             cols = slice(b * P, (b + 1) * P)
-            for a in range(PASSES):
-                nc.tensor.matmul_mx(
-                    out=bank[:],
-                    lhsT=v_w[a, u][:, cols].bitcast(E4M3),
-                    lhsT_scale=v_s[a, u][:, cols],
-                    rhs=codes[a],
-                    rhs_scale=scales[a],
-                    start=(a == 0),
-                    stop=(a == PASSES - 1),
-                )
+            nc.tensor.matmul_mx(
+                out=bank[:],
+                lhsT=v_w[a, u][:, cols].bitcast(E4M3),
+                lhsT_scale=v_s[a, u][:, cols],
+                rhs=codes,
+                rhs_scale=scales,
+                start=(a == 0),
+                stop=(a == PASSES - 1),
+            )
+
+        def dealt(bank):
             return bank[:].rearrange("j (m t) -> j t m", t=PACK)
 
         def by_tile(tile):
             return tile[:].rearrange("j (t m) -> j t m", t=PACK)
 
-        bent = {}
-        third = {}
-        for u in range(HALVES):
-            for b in range(BLOCKS):
-                bent[u, b] = staged("bent")
-                third[u, b] = staged("third")
-                sums = product(u, b, [w2_w[:, a, :].bitcast(E2M1) for a in range(PASSES)], [w2_s[:, a, :] for a in range(PASSES)])
-                nc.scalar.activation(by_tile(bent[u, b]), sums, ACT.Tanh)
-                sums = product(u, b, [w3_w[:, a, :].bitcast(E4M3) for a in range(PASSES)], [w3_s[:, a, :] for a in range(PASSES)])
-                nc.scalar.copy(by_tile(third[u, b]), sums)
-
         w1_c = []
         w1_s = []
-        for a in range(PASSES):
+
+        def quantise_w1(a):
             woven = ring.tile([P, H, PACK], BF16, name="woven", tag="woven", align_bytes=64)
-            dst = woven[:].rearrange("p (c e) i -> p c i e", e=4)
-            src = w1_raw[a][:].rearrange("p i (c e) -> p c i e", e=4)
-            if a == 0:
-                nc.scalar.copy(dst, src)
-            else:
-                nc.vector.tensor_copy(dst, src)
+            nc.vector.tensor_copy(
+                woven[:].rearrange("p (c e) i -> p c i e", e=4),
+                w1_raw[a][:].rearrange("p i (c e) -> p c i e", e=4),
+            )
             w1_c.append(held([P, H], U32, "w1_c%d" % a))
             w1_s.append(held([P, H], U8, "w1_s%d" % a))
             nc.vector.quantize_mx(out=w1_c[a][:].bitcast(E4M3), scales=w1_s[a][:], in_=woven[:].rearrange("p n i -> p (n i)"))
 
-        fresh = [held([P, S], F32, "fresh%d" % t) for t in range(PACK)]
-
-        def turn(t, u):
-            bank = psum.tile([P, BANK], F32, name="turned", tag="turned", bufs=2)
-            rows = slice(t * P, (t + 1) * P)
-            for b in range(BLOCKS):
-                cols = slice(b * P, (b + 1) * P)
-                nc.tensor.matmul(bank[:, cols], lhsT=bent[u, b][:, rows], rhs=ident[:], is_transpose=True, start=True, stop=False)
-                nc.tensor.matmul(bank[:, cols], lhsT=third[u, b][:, rows], rhs=ident[:], is_transpose=True, start=False, stop=True)
-            nc.scalar.copy(fresh[t][:, u * BANK : (u + 1) * BANK], bank[:])
-
         for u in range(HALVES):
+            for a in range(PASSES):
+                gather_words(a, u)
+            if u == 0:
+                for v in range(HALVES):
+                    for a in range(PASSES):
+                        gather_scales(a, v)
+            bent = []
+            third = []
             for b in range(BLOCKS):
-                sums = product(u, b, [w1_c[a][:].bitcast(E4M3) for a in range(PASSES)], [w1_s[a][:] for a in range(PASSES)])
-                nc.vector.tensor_tensor(by_tile(bent[u, b]), sums, by_tile(bent[u, b]), ALU.mult)
-            turn(0, u)
-        for t in range(1, PACK):
-            for u in range(HALVES):
-                turn(t, u)
-
-        def replace(t, first, last):
-            nc.vector.tensor_tensor(
-                page[t][:].indirect(put[:, first // 16 : last // 16]),
-                fresh[t][:, first:last],
-                gain[t][:, first:last],
-                ALU.mult,
-            )
+                bent.append(staged("bent", BANK))
+                third.append(staged("third", BANK))
+                bank = mx_bank()
+                for a in range(PASSES):
+                    one_pass(bank, u, b, a, w2_w[:, a, :].bitcast(E2M1), w2_s[:, a, :])
+                nc.scalar.activation(by_tile(bent[b]), dealt(bank), ACT.Tanh)
+                bank = mx_bank()
+                for a in range(PASSES):
+                    one_pass(bank, u, b, a, w3_w[:, a, :].bitcast(E4M3), w3_s[:, a, :])
+                nc.scalar.copy(by_tile(third[b]), dealt(bank))
+            if u == 0:
+                for a in range(PASSES):
+                    quantise_w1(a)
+            banks = [mx_bank() for b in range(BLOCKS)]
+            for a in range(PASSES):
+                for b in range(BLOCKS):
+                    one_pass(banks[b], u, b, a, w1_c[a][:].bitcast(E4M3), w1_s[a][:])
+            term = []
+            for b in range(BLOCKS):
+                tag = "term%d" % b if u == 0 else ("gain10", "fresh10", "gain20", "fresh20")[b]
+                term.append(keep.tile([P, BANK], F32, name="term", tag=tag))
+                nc.vector.tensor_tensor(by_tile(term[b]), dealt(banks[b]), by_tile(bent[b]), ALU.mult)
+            for t in range(PACK):
+                turned = psum.tile([P, BANK], F32, name="turned", tag="turned", bufs=2)
+                rows = slice(t * P, (t + 1) * P)
+                for b in range(BLOCKS):
+                    cols = slice(b * P, (b + 1) * P)
+                    nc.tensor.matmul(turned[:, cols], lhsT=third[b][:, rows], rhs=ident[:], is_transpose=True, start=True, stop=False)
+                    nc.tensor.matmul(turned[:, cols], lhsT=term[b][:, rows], rhs=ident[:], is_transpose=True, start=False, stop=True)
+                fresh = keep.tile([P, BANK], F32, name="fresh", tag="fresh%d%d" % (t, u))
+                nc.scalar.copy(fresh[:], turned[:])
+                nc.vector.tensor_tensor(page[t][:].indirect(put[:, u * 32 : (u + 1) * 32]), fresh[:], gain[t, u], ALU.mult)
 
         w4_raw = ring.tile([P, PACK, H], F32, name="w4_raw", tag="raw")
         nc.sync.dma_start(out=w4_raw[:], in_=w4.rearrange("(p i) n -> p i n", i=PACK))
@@ -189,12 +199,8 @@ def tile_list_leave_ledger_exchange_kernel(
         w4_c = held([P, H], U32, "w4_c")
         w4_s = held([P, H], U8, "w4_s")
 
-        rounded = [held([P, BANK, PACK], BF16, "rounded%d" % c) for c in range(SPANS)]
+        rounded = [held([P, last - first, PACK], BF16, "rounded%d" % first) for first, last in SPANS]
 
-        for u in range(HALVES):
-            replace(0, u * BANK, (u + 1) * BANK)
-        for t in range(1, PACK):
-            replace(t, 0, S)
         for t in range(PACK):
             kept = ring.tile([P, PAIRS], F32, name="kept")
             swapped = ring.tile([P, PAIRS], F32, name="swapped")
@@ -208,30 +214,22 @@ def tile_list_leave_ledger_exchange_kernel(
             nc.vector.tensor_tensor(low[:], kept[:], swapped[:], ALU.min)
             nc.vector.tensor_copy(page[t][:].indirect(larger[:]), high[:])
             nc.vector.tensor_copy(page[t][:].indirect(smaller[:]), low[:])
-            for c in range(SPANS):
-                nc.scalar.copy(rounded[c][:, :, t], page[t][:, c * BANK : (c + 1) * BANK])
+            for c, (first, last) in enumerate(SPANS):
+                nc.scalar.copy(rounded[c][:, :, t], page[t][:, first:last])
 
         out_rows = out.rearrange("(p t) c -> p t c", t=PACK)
-        b_c = {}
-        b_s = {}
-
-        def quantise(c):
-            b_c[c] = held([P, BANK], U32, "b_c%d" % c)
-            b_s[c] = held([P, BANK], U8, "b_s%d" % c)
-            nc.vector.quantize_mx(out=b_c[c][:].bitcast(E4M3), scales=b_s[c][:], in_=rounded[c][:].rearrange("p n i -> p (n i)"))
-
-        quantise(0)
-        for c in range(SPANS):
-            cols = slice(c * BANK, (c + 1) * BANK)
-            if c + 1 < SPANS:
-                quantise(c + 1)
+        for c, (first, last) in enumerate(SPANS):
+            width = last - first
+            b_c = held([P, width], U32, "b_c%d" % c)
+            b_s = held([P, width], U8, "b_s%d" % c)
+            nc.vector.quantize_mx(out=b_c[:].bitcast(E4M3), scales=b_s[:], in_=rounded[c][:].rearrange("p n i -> p (n i)"))
             for t in range(PACK):
                 rows = slice(t * P, (t + 1) * P)
-                bank = psum.tile([P, BANK], F32, name="bank", tag="mx", bufs=6)
+                bank = mx_bank()
                 nc.tensor.matmul_mx(
-                    out=bank[:], lhsT=w4_c[:, rows].bitcast(E4M3), lhsT_scale=w4_s[:, rows],
-                    rhs=b_c[c][:].bitcast(E4M3), rhs_scale=b_s[c][:], start=True, stop=True,
+                    out=bank[:, 0:width], lhsT=w4_c[:, rows].bitcast(E4M3), lhsT_scale=w4_s[:, rows],
+                    rhs=b_c[:].bitcast(E4M3), rhs_scale=b_s[:], start=True, stop=True,
                 )
-                result = staged("result")
-                nc.vector.scalar_tensor_tensor(result[:], page[t][:, cols], skip_t[:, t : t + 1], bank[:], ALU.mult, ALU.add)
-                nc.sync.dma_start(out=out_rows[:, t, cols], in_=result[:])
+                result = staged("result", width)
+                nc.vector.scalar_tensor_tensor(result[:], page[t][:, first:last], skip_t[:, t : t + 1], bank[:, 0:width], ALU.mult, ALU.add)
+                nc.sync.dma_start(out=out_rows[:, t, first:last], in_=result[:])

@@ -47,9 +47,9 @@ def tile_list_leave_ledger_exchange_kernel(
             nc.sync.dma_start(tile[:], src)
             return tile
 
-        def load_scales(queue, zeroer, src, name):
+        def load_scales(queue, src, name):
             tile = held([P, PASSES, src.shape[2]], U8, name)
-            zeroer.memset(tile[:].bitcast(I32), 0)
+            nc.vector.memset(tile[:].bitcast(I32), 0)
             for q in range(4):
                 queue.dma_start(
                     out=tile[32 * q : 32 * q + 4, :, :].bitcast(I32),
@@ -57,28 +57,32 @@ def tile_list_leave_ledger_exchange_kernel(
                 )
             return tile
 
+        def load_rows(rows):
+            tile = ring.tile([P, PACK, H], F32, name="raw", tag="raw")
+            nc.sync.dma_start(out=tile[:], in_=rows.rearrange("(p i) n -> p i n", i=PACK))
+            return tile
+
         def load_words(a):
             tile = held([P, T], I32, "tab_w%d" % a)
             nc.sync.dma_start(out=tile[:], in_=tab_words[a].rearrange("p t i -> p (t i)").bitcast(I32))
             return tile
 
+        w2_s = load_scales(nc.scalar, w2_scales, "w2_s")
+        w3_s = load_scales(nc.gpsimd, w3_scales, "w3_s")
         ident = held([P, P], F32, "ident")
         make_identity(nc, ident[:])
-
         pick = load_list(offs, "pick")
+        tab_s = held([P, T], U8, "tab_s")
+        nc.sync.dma_start(out=tab_s[0:32, :].bitcast(I32), in_=tab_scales.rearrange("a q n -> (a q) n").bitcast(I32))
+        nc.vector.memset(tab_s[32:64, :].bitcast(I32), 0)
+        nc.vector.memset(tab_s[64:128, :].bitcast(I32), 0)
         tab_w = [load_words(a) for a in range(PASSES)]
-        tab_s = load_scales(nc.sync, nc.vector, tab_scales, "tab_s")
         w2_w = held([P, PASSES, 2 * H], U8, "w2_w")
         nc.sync.dma_start(out=w2_w[:].bitcast(I32), in_=w2_words.rearrange("a p n -> p a n").bitcast(I32))
-        w2_s = load_scales(nc.sync, nc.gpsimd, w2_scales, "w2_s")
+        w1_raw = [load_rows(w1[0:512, :])]
         w3_w = held([P, PASSES, H], I32, "w3_w")
         nc.sync.dma_start(out=w3_w[:], in_=w3_words.rearrange("a p n i -> p a (n i)").bitcast(I32))
-        w3_s = load_scales(nc.sync, nc.gpsimd, w3_scales, "w3_s")
-        w1_raw = []
-        for a in range(PASSES):
-            tile = ring.tile([P, PACK, H], F32, name="w1_raw%d" % a, tag="raw")
-            nc.sync.dma_start(out=tile[:], in_=w1[a * 512 : (a + 1) * 512, :].rearrange("(p i) n -> p i n", i=PACK))
-            w1_raw.append(tile)
+        w1_raw.append(load_rows(w1[512:1024, :]))
         put = load_list(offs2, "put")
         wgs_rows = wgs.rearrange("(m t) j -> m t j", t=PACK)
         page_rows = page0.rearrange("(p t) c -> p t c", t=PACK)
@@ -99,31 +103,39 @@ def tile_list_leave_ledger_exchange_kernel(
         larger = load_list(offs3, "larger")
         smaller = load_list(offs4, "smaller")
 
+        picked_s = held([P, S], U8, "picked_s")
+        nc.vector.tensor_copy(picked_s[:], tab_s[:].indirect(pick[:]))
+        v_s = held([P, PASSES, S], U8, "v_s")
+        nc.vector.memset(v_s[:].bitcast(I32), 0)
+        for a in range(PASSES):
+            for q in range(4):
+                nc.scalar.dma_start(
+                    out=v_s[32 * q : 32 * q + 4, a, :].bitcast(I32),
+                    in_=picked_s[16 * a + 4 * q : 16 * a + 4 * q + 4, :].bitcast(I32),
+                )
         v_w = {}
-        v_s = {}
-
-        def gather_words(a, u):
-            v_w[a, u] = ring.tile([P, BANK], U32, name="v_w%d" % a, tag="v_w%d" % a, bufs=PASSES - a, align_bytes=64)
-            nc.vector.tensor_copy(v_w[a, u][:], tab_w[a][:].bitcast(U32).indirect(pick[:, u * 32 : (u + 1) * 32]))
-
-        def gather_scales(a, u):
-            v_s[a, u] = held([P, BANK], U8, "v_s%d%d" % (a, u))
-            nc.vector.tensor_copy(v_s[a, u][:], tab_s[:, a, :].indirect(pick[:, u * 32 : (u + 1) * 32]))
+        for u in range(HALVES):
+            for a in range(PASSES):
+                v_w[a, u] = held([P, BANK], U32, "v_w%d%d" % (a, u))
+                nc.vector.tensor_copy(v_w[a, u][:], tab_w[a][:].bitcast(U32).indirect(pick[:, u * 32 : (u + 1) * 32]))
 
         def mx_bank():
             return psum.tile([P, BANK], F32, name="bank", tag="mx", bufs=6)
 
-        def one_pass(bank, u, b, a, codes, scales):
-            cols = slice(b * P, (b + 1) * P)
-            nc.tensor.matmul_mx(
-                out=bank[:],
-                lhsT=v_w[a, u][:, cols].bitcast(E4M3),
-                lhsT_scale=v_s[a, u][:, cols],
-                rhs=codes,
-                rhs_scale=scales,
-                start=(a == 0),
-                stop=(a == PASSES - 1),
-            )
+        def product(u, codes, scales):
+            banks = [mx_bank() for b in range(BLOCKS)]
+            for a in range(PASSES):
+                for b in range(BLOCKS):
+                    nc.tensor.matmul_mx(
+                        out=banks[b][:],
+                        lhsT=v_w[a, u][:, b * P : (b + 1) * P].bitcast(E4M3),
+                        lhsT_scale=v_s[:, a, u * BANK + b * P : u * BANK + (b + 1) * P],
+                        rhs=codes[a],
+                        rhs_scale=scales[a],
+                        start=(a == 0),
+                        stop=(a == PASSES - 1),
+                    )
+            return banks
 
         def dealt(bank):
             return bank[:].rearrange("j (m t) -> j t m", t=PACK)
@@ -145,32 +157,18 @@ def tile_list_leave_ledger_exchange_kernel(
             nc.vector.quantize_mx(out=w1_c[a][:].bitcast(E4M3), scales=w1_s[a][:], in_=woven[:].rearrange("p n i -> p (n i)"))
 
         for u in range(HALVES):
-            for a in range(PASSES):
-                gather_words(a, u)
-            if u == 0:
-                for v in range(HALVES):
-                    for a in range(PASSES):
-                        gather_scales(a, v)
-            bent = []
-            third = []
+            bent = [staged("bent", BANK) for b in range(BLOCKS)]
+            third = [staged("third", BANK) for b in range(BLOCKS)]
+            banks = product(u, [w2_w[:, a, :].bitcast(E2M1) for a in range(PASSES)], [w2_s[:, a, :] for a in range(PASSES)])
             for b in range(BLOCKS):
-                bent.append(staged("bent", BANK))
-                third.append(staged("third", BANK))
-                bank = mx_bank()
-                for a in range(PASSES):
-                    one_pass(bank, u, b, a, w2_w[:, a, :].bitcast(E2M1), w2_s[:, a, :])
-                nc.scalar.activation(by_tile(bent[b]), dealt(bank), ACT.Tanh)
-                bank = mx_bank()
-                for a in range(PASSES):
-                    one_pass(bank, u, b, a, w3_w[:, a, :].bitcast(E4M3), w3_s[:, a, :])
-                nc.scalar.copy(by_tile(third[b]), dealt(bank))
+                nc.scalar.activation(by_tile(bent[b]), dealt(banks[b]), ACT.Tanh)
+            banks = product(u, [w3_w[:, a, :].bitcast(E4M3) for a in range(PASSES)], [w3_s[:, a, :] for a in range(PASSES)])
+            for b in range(BLOCKS):
+                nc.scalar.copy(by_tile(third[b]), dealt(banks[b]))
             if u == 0:
                 for a in range(PASSES):
                     quantise_w1(a)
-            banks = [mx_bank() for b in range(BLOCKS)]
-            for a in range(PASSES):
-                for b in range(BLOCKS):
-                    one_pass(banks[b], u, b, a, w1_c[a][:].bitcast(E4M3), w1_s[a][:])
+            banks = product(u, [w1_c[a][:].bitcast(E4M3) for a in range(PASSES)], [w1_s[a][:] for a in range(PASSES)])
             term = []
             for b in range(BLOCKS):
                 tag = "term%d" % b if u == 0 else ("gain10", "fresh10", "gain20", "fresh20")[b]
@@ -187,8 +185,7 @@ def tile_list_leave_ledger_exchange_kernel(
                 nc.scalar.copy(fresh[:], turned[:])
                 nc.vector.tensor_tensor(page[t][:].indirect(put[:, u * 32 : (u + 1) * 32]), fresh[:], gain[t, u], ALU.mult)
 
-        w4_raw = ring.tile([P, PACK, H], F32, name="w4_raw", tag="raw")
-        nc.sync.dma_start(out=w4_raw[:], in_=w4.rearrange("(p i) n -> p i n", i=PACK))
+        w4_raw = load_rows(w4)
         skip_t = held([P, PACK], F32, "skip_t")
         nc.sync.dma_start(out=skip_t[:], in_=skip.rearrange("(p t) -> p t", t=PACK))
         w4_woven = ring.tile([P, H, PACK], BF16, name="w4_woven", tag="woven", align_bytes=64)

@@ -109,7 +109,7 @@ def tile_list_leave_ledger_exchange_kernel(
         nc.vector.memset(v_s[:].bitcast(I32), 0)
         for a in range(PASSES):
             for q in range(4):
-                nc.scalar.dma_start(
+                (nc.scalar, nc.gpsimd)[a].dma_start(
                     out=v_s[32 * q : 32 * q + 4, a, :].bitcast(I32),
                     in_=picked_s[16 * a + 4 * q : 16 * a + 4 * q + 4, :].bitcast(I32),
                 )
@@ -175,15 +175,19 @@ def tile_list_leave_ledger_exchange_kernel(
                 term.append(keep.tile([P, BANK], F32, name="term", tag=tag))
                 nc.vector.tensor_tensor(by_tile(term[b]), dealt(banks[b]), by_tile(bent[b]), ALU.mult)
             for t in range(PACK):
-                turned = psum.tile([P, BANK], F32, name="turned", tag="turned", bufs=2)
                 rows = slice(t * P, (t + 1) * P)
-                for b in range(BLOCKS):
-                    cols = slice(b * P, (b + 1) * P)
-                    nc.tensor.matmul(turned[:, cols], lhsT=third[b][:, rows], rhs=ident[:], is_transpose=True, start=True, stop=False)
-                    nc.tensor.matmul(turned[:, cols], lhsT=term[b][:, rows], rhs=ident[:], is_transpose=True, start=False, stop=True)
                 fresh = keep.tile([P, BANK], F32, name="fresh", tag="fresh%d%d" % (t, u))
-                nc.scalar.copy(fresh[:], turned[:])
-                nc.vector.tensor_tensor(page[t][:].indirect(put[:, u * 32 : (u + 1) * 32]), fresh[:], gain[t, u], ALU.mult)
+                step = BLOCKS // 2 if (t, u) == (0, 0) else BLOCKS
+                for b0 in range(0, BLOCKS, step):
+                    turned = psum.tile([P, step * P], F32, name="turned", tag="turned", bufs=2)
+                    for b in range(step):
+                        cols = slice(b * P, (b + 1) * P)
+                        nc.tensor.matmul(turned[:, cols], lhsT=third[b0 + b][:, rows], rhs=ident[:], is_transpose=True, start=True, stop=False)
+                        nc.tensor.matmul(turned[:, cols], lhsT=term[b0 + b][:, rows], rhs=ident[:], is_transpose=True, start=False, stop=True)
+                    part = slice(b0 * P, (b0 + step) * P)
+                    nc.scalar.copy(fresh[:, part], turned[:])
+                    entries = put[:, (u * BANK + part.start) // 16 : (u * BANK + part.stop) // 16]
+                    nc.vector.tensor_tensor(page[t][:].indirect(entries), fresh[:, part], gain[t, u][:, part], ALU.mult)
 
         w4_raw = load_rows(w4)
         skip_t = held([P, PACK], F32, "skip_t")

@@ -19,10 +19,16 @@ ACT = mybir.ActivationFunctionType
 
 P = 128
 PACK = 4
-PASSES = K // (P * PACK)
+K_PASS = P * PACK
+PASSES = K // K_PASS
+QUADRANTS = 4
 BANK = 512
 HALVES = S // BANK
 BLOCKS = BANK // P
+PER_COLUMN = 16
+LINE = 4
+MX_BANKS, TURN_BANKS = 6, 2
+STAGED = 2 * HALVES * BLOCKS
 SPANS = [(0, 256), (256, 512), (512, 1024), (1024, 1536), (1536, 2048)]
 
 
@@ -40,7 +46,7 @@ def tile_list_leave_ledger_exchange_kernel(
             return keep.tile(shape, dtype, name=name, align_bytes=64)
 
         def staged(name, width):
-            return ring.tile([P, width], F32, name=name, tag="staged", bufs=16)
+            return ring.tile([P, width], F32, name=name, tag="staged", bufs=STAGED)
 
         def load_list(src, name):
             tile = keep.tile([P, src.shape[1]], U16, name=name)
@@ -50,7 +56,7 @@ def tile_list_leave_ledger_exchange_kernel(
         def load_scales(queue, src, name):
             tile = held([P, PASSES, src.shape[2]], U8, name)
             nc.vector.memset(tile[:].bitcast(I32), 0)
-            for q in range(4):
+            for q in range(QUADRANTS):
                 queue.dma_start(
                     out=tile[32 * q : 32 * q + 4, :, :].bitcast(I32),
                     in_=src[:, 4 * q : 4 * q + 4, :].rearrange("a r n -> r a n").bitcast(I32),
@@ -79,10 +85,10 @@ def tile_list_leave_ledger_exchange_kernel(
         tab_w = [load_words(a) for a in range(PASSES)]
         w2_w = held([P, PASSES, 2 * H], U8, "w2_w")
         nc.sync.dma_start(out=w2_w[:].bitcast(I32), in_=w2_words.rearrange("a p n -> p a n").bitcast(I32))
-        w1_raw = [load_rows(w1[0:512, :])]
+        w1_raw = [load_rows(w1[0:K_PASS, :])]
         w3_w = held([P, PASSES, H], I32, "w3_w")
         nc.sync.dma_start(out=w3_w[:], in_=w3_words.rearrange("a p n i -> p a (n i)").bitcast(I32))
-        w1_raw.append(load_rows(w1[512:1024, :]))
+        w1_raw.append(load_rows(w1[K_PASS:K, :]))
         put = load_list(offs2, "put")
         wgs_rows = wgs.rearrange("(m t) j -> m t j", t=PACK)
         page_rows = page0.rearrange("(p t) c -> p t c", t=PACK)
@@ -91,7 +97,7 @@ def tile_list_leave_ledger_exchange_kernel(
 
         def load_gain(first, last, u):
             tile = keep.tile([P, last - first, BANK], F32, name="gain", tag="gain%d%d" % (first, u))
-            for q in range(4):
+            for q in range(QUADRANTS):
                 nc.sync.dma_start(out=tile[32 * q : 32 * q + 32, :, :], in_=wgs_rows[:, first:last, u * BANK : (u + 1) * BANK])
             for t in range(first, last):
                 gain[t, u] = tile[:, t - first, :]
@@ -105,22 +111,28 @@ def tile_list_leave_ledger_exchange_kernel(
 
         picked_s = held([P, S], U8, "picked_s")
         nc.vector.tensor_copy(picked_s[:], tab_s[:].indirect(pick[:]))
-        v_s = held([P, PASSES, S], U8, "v_s")
-        nc.vector.memset(v_s[:].bitcast(I32), 0)
-        for a in range(PASSES):
-            for q in range(4):
-                (nc.scalar, nc.gpsimd)[a].dma_start(
-                    out=v_s[32 * q : 32 * q + 4, a, :].bitcast(I32),
+        v_s = []
+        for a, queue in enumerate((nc.scalar, nc.gpsimd)):
+            v_s.append(held([P, S], U8, "v_s%d" % a))
+            nc.vector.memset(v_s[a][:].bitcast(I32), 0)
+            for q in range(QUADRANTS):
+                queue.dma_start(
+                    out=v_s[a][32 * q : 32 * q + 4, :].bitcast(I32),
                     in_=picked_s[16 * a + 4 * q : 16 * a + 4 * q + 4, :].bitcast(I32),
                 )
+
+        def entries(listed, first, last):
+            return listed[:, first // PER_COLUMN : last // PER_COLUMN]
+
         v_w = {}
         for u in range(HALVES):
             for a in range(PASSES):
                 v_w[a, u] = held([P, BANK], U32, "v_w%d%d" % (a, u))
-                nc.vector.tensor_copy(v_w[a, u][:], tab_w[a][:].bitcast(U32).indirect(pick[:, u * 32 : (u + 1) * 32]))
+                window = tab_w[a][:].bitcast(U32)
+                nc.vector.tensor_copy(v_w[a, u][:], window.indirect(entries(pick, u * BANK, (u + 1) * BANK)))
 
         def mx_bank():
-            return psum.tile([P, BANK], F32, name="bank", tag="mx", bufs=6)
+            return psum.tile([P, BANK], F32, name="bank", tag="mx", bufs=MX_BANKS)
 
         def product(u, codes, scales):
             banks = [mx_bank() for b in range(BLOCKS)]
@@ -129,7 +141,7 @@ def tile_list_leave_ledger_exchange_kernel(
                     nc.tensor.matmul_mx(
                         out=banks[b][:],
                         lhsT=v_w[a, u][:, b * P : (b + 1) * P].bitcast(E4M3),
-                        lhsT_scale=v_s[:, a, u * BANK + b * P : u * BANK + (b + 1) * P],
+                        lhsT_scale=v_s[a][:, u * BANK + b * P : u * BANK + (b + 1) * P],
                         rhs=codes[a],
                         rhs_scale=scales[a],
                         start=(a == 0),
@@ -149,12 +161,14 @@ def tile_list_leave_ledger_exchange_kernel(
         def quantise_w1(a):
             woven = ring.tile([P, H, PACK], BF16, name="woven", tag="woven", align_bytes=64)
             nc.vector.tensor_copy(
-                woven[:].rearrange("p (c e) i -> p c i e", e=4),
-                w1_raw[a][:].rearrange("p i (c e) -> p c i e", e=4),
+                woven[:].rearrange("p (c e) i -> p c i e", e=LINE),
+                w1_raw[a][:].rearrange("p i (c e) -> p c i e", e=LINE),
             )
             w1_c.append(held([P, H], U32, "w1_c%d" % a))
             w1_s.append(held([P, H], U8, "w1_s%d" % a))
             nc.vector.quantize_mx(out=w1_c[a][:].bitcast(E4M3), scales=w1_s[a][:], in_=woven[:].rearrange("p n i -> p (n i)"))
+
+        term_tags = [["term%d" % b for b in range(BLOCKS)], ["gain10", "fresh10", "gain20", "fresh20"]]
 
         for u in range(HALVES):
             bent = [staged("bent", BANK) for b in range(BLOCKS)]
@@ -171,23 +185,22 @@ def tile_list_leave_ledger_exchange_kernel(
             banks = product(u, [w1_c[a][:].bitcast(E4M3) for a in range(PASSES)], [w1_s[a][:] for a in range(PASSES)])
             term = []
             for b in range(BLOCKS):
-                tag = "term%d" % b if u == 0 else ("gain10", "fresh10", "gain20", "fresh20")[b]
-                term.append(keep.tile([P, BANK], F32, name="term", tag=tag))
+                term.append(keep.tile([P, BANK], F32, name="term", tag=term_tags[u][b]))
                 nc.vector.tensor_tensor(by_tile(term[b]), dealt(banks[b]), by_tile(bent[b]), ALU.mult)
             for t in range(PACK):
                 rows = slice(t * P, (t + 1) * P)
                 fresh = keep.tile([P, BANK], F32, name="fresh", tag="fresh%d%d" % (t, u))
                 step = BLOCKS // 2 if (t, u) == (0, 0) else BLOCKS
                 for b0 in range(0, BLOCKS, step):
-                    turned = psum.tile([P, step * P], F32, name="turned", tag="turned", bufs=2)
+                    turned = psum.tile([P, step * P], F32, name="turned", tag="turned", bufs=TURN_BANKS)
                     for b in range(step):
                         cols = slice(b * P, (b + 1) * P)
                         nc.tensor.matmul(turned[:, cols], lhsT=third[b0 + b][:, rows], rhs=ident[:], is_transpose=True, start=True, stop=False)
                         nc.tensor.matmul(turned[:, cols], lhsT=term[b0 + b][:, rows], rhs=ident[:], is_transpose=True, start=False, stop=True)
                     part = slice(b0 * P, (b0 + step) * P)
                     nc.scalar.copy(fresh[:, part], turned[:])
-                    entries = put[:, (u * BANK + part.start) // 16 : (u * BANK + part.stop) // 16]
-                    nc.vector.tensor_tensor(page[t][:].indirect(entries), fresh[:, part], gain[t, u][:, part], ALU.mult)
+                    places = entries(put, u * BANK + part.start, u * BANK + part.stop)
+                    nc.vector.tensor_tensor(page[t][:].indirect(places), fresh[:, part], gain[t, u][:, part], ALU.mult)
 
         w4_raw = load_rows(w4)
         skip_t = held([P, PACK], F32, "skip_t")
@@ -221,15 +234,15 @@ def tile_list_leave_ledger_exchange_kernel(
         out_rows = out.rearrange("(p t) c -> p t c", t=PACK)
         for c, (first, last) in enumerate(SPANS):
             width = last - first
-            b_c = held([P, width], U32, "b_c%d" % c)
-            b_s = held([P, width], U8, "b_s%d" % c)
-            nc.vector.quantize_mx(out=b_c[:].bitcast(E4M3), scales=b_s[:], in_=rounded[c][:].rearrange("p n i -> p (n i)"))
+            page_c = held([P, width], U32, "page_c%d" % c)
+            page_s = held([P, width], U8, "page_s%d" % c)
+            nc.vector.quantize_mx(out=page_c[:].bitcast(E4M3), scales=page_s[:], in_=rounded[c][:].rearrange("p n i -> p (n i)"))
             for t in range(PACK):
                 rows = slice(t * P, (t + 1) * P)
                 bank = mx_bank()
                 nc.tensor.matmul_mx(
                     out=bank[:, 0:width], lhsT=w4_c[:, rows].bitcast(E4M3), lhsT_scale=w4_s[:, rows],
-                    rhs=b_c[:].bitcast(E4M3), rhs_scale=b_s[:], start=True, stop=True,
+                    rhs=page_c[:].bitcast(E4M3), rhs_scale=page_s[:], start=True, stop=True,
                 )
                 result = staged("result", width)
                 nc.vector.scalar_tensor_tensor(result[:], page[t][:, first:last], skip_t[:, t : t + 1], bank[:, 0:width], ALU.mult, ALU.add)

from contextlib import ExitStack

import concourse.mybir as mybir
from concourse.masks import make_identity

K, H, T, S, T2, PAIRS = 1024, 512, 2048, 1024, 2048, 512
FLOPS = 2 * (3 * K * H * S + H * H * T2)

F32 = mybir.dt.float32
BF16 = mybir.dt.bfloat16
I32 = mybir.dt.int32
U32 = mybir.dt.uint32
U16 = mybir.dt.uint16
U8 = mybir.dt.uint8
E4M3 = mybir.dt.float8_e4m3fn_x4
E2M1 = mybir.dt.float4_e2m1fn_x4
ALU = mybir.AluOpType
ACT = mybir.ActivationFunctionType

P = 128
PACK = 4
K_PASS = P * PACK
PASSES = K // K_PASS
QUADRANTS = 4
BANK = 512
HALVES = S // BANK
BLOCKS = BANK // P
PER_COLUMN = 16
LINE = 4
MX_BANKS, TURN_BANKS = 6, 2
STAGED = 2 * HALVES * BLOCKS
SPANS = [(0, 256), (256, 512), (512, 1024), (1024, 1536), (1536, 2048)]


def tile_list_leave_ledger_exchange_kernel(
    tc, tab_words, tab_scales, offs, w1, w2_words, w2_scales, w3_words, w3_scales,
    page0, wgs, offs2, offs3, offs4, w4, skip, out,
):
    nc = tc.nc
    with ExitStack() as ctx:
        keep = ctx.enter_context(tc.tile_pool(name="keep", bufs=1))
        ring = ctx.enter_context(tc.tile_pool(name="ring", bufs=2))
        psum = ctx.enter_context(tc.psum_pool(name="psum", bufs=1))

        def held(shape, dtype, name):
            return keep.tile(shape, dtype, name=name, align_bytes=64)

        def staged(name, width):
            return ring.tile([P, width], F32, name=name, tag="staged", bufs=STAGED)

        def load_list(src, name):
            tile = keep.tile([P, src.shape[1]], U16, name=name)
            nc.sync.dma_start(tile[:], src)
            return tile

        def load_scales(queue, src, name):
            tile = held([P, PASSES, src.shape[2]], U8, name)
            nc.vector.memset(tile[:].bitcast(I32), 0)
            for q in range(QUADRANTS):
                queue.dma_start(
                    out=tile[32 * q : 32 * q + 4, :, :].bitcast(I32),
                    in_=src[:, 4 * q : 4 * q + 4, :].rearrange("a r n -> r a n").bitcast(I32),
                )
            return tile

        def load_rows(rows):
            tile = ring.tile([P, PACK, H], F32, name="raw", tag="raw")
            nc.sync.dma_start(out=tile[:], in_=rows.rearrange("(p i) n -> p i n", i=PACK))
            return tile

        def load_words(a):
            tile = held([P, T], I32, "tab_w%d" % a)
            nc.sync.dma_start(out=tile[:], in_=tab_words[a].rearrange("p t i -> p (t i)").bitcast(I32))
            return tile

        w2_s = load_scales(nc.scalar, w2_scales, "w2_s")
        w3_s = load_scales(nc.gpsimd, w3_scales, "w3_s")
        ident = held([P, P], F32, "ident")
        make_identity(nc, ident[:])
        pick = load_list(offs, "pick")
        tab_s = held([P, T], U8, "tab_s")
        nc.sync.dma_start(out=tab_s[0:32, :].bitcast(I32), in_=tab_scales.rearrange("a q n -> (a q) n").bitcast(I32))
        nc.vector.memset(tab_s[32:64, :].bitcast(I32), 0)
        nc.vector.memset(tab_s[64:128, :].bitcast(I32), 0)
        tab_w = [load_words(a) for a in range(PASSES)]
        w2_w = held([P, PASSES, 2 * H], U8, "w2_w")
        nc.sync.dma_start(out=w2_w[:].bitcast(I32), in_=w2_words.rearrange("a p n -> p a n").bitcast(I32))
        w1_raw = [load_rows(w1[0:K_PASS, :])]
        w3_w = held([P, PASSES, H], I32, "w3_w")
        nc.sync.dma_start(out=w3_w[:], in_=w3_words.rearrange("a p n i -> p a (n i)").bitcast(I32))
        w1_raw.append(load_rows(w1[K_PASS:K, :]))
        put = load_list(offs2, "put")
        wgs_rows = wgs.rearrange("(m t) j -> m t j", t=PACK)
        page_rows = page0.rearrange("(p t) c -> p t c", t=PACK)
        page = [held([P, T2], F32, "page%d" % t) for t in range(PACK)]
        gain = {}

        def load_gain(first, last, u):
            tile = keep.tile([P, last - first, BANK], F32, name="gain", tag="gain%d%d" % (first, u))
            for q in range(QUADRANTS):
                nc.sync.dma_start(out=tile[32 * q : 32 * q + 32, :, :], in_=wgs_rows[:, first:last, u * BANK : (u + 1) * BANK])
            for t in range(first, last):
                gain[t, u] = tile[:, t - first, :]

        for t in range(PACK):
            load_gain(t, t + 1, 0)
            nc.sync.dma_start(out=page[t][:], in_=page_rows[:, t, :])
        load_gain(0, PACK, 1)
        larger = load_list(offs3, "larger")
        smaller = load_list(offs4, "smaller")

        picked_s = held([P, S], U8, "picked_s")
        nc.vector.tensor_copy(picked_s[:], tab_s[:].indirect(pick[:]))
        v_s = []
        for a, queue in enumerate((nc.scalar, nc.gpsimd)):
            v_s.append(held([P, S], U8, "v_s%d" % a))
            nc.vector.memset(v_s[a][:].bitcast(I32), 0)
            for q in range(QUADRANTS):
                queue.dma_start(
                    out=v_s[a][32 * q : 32 * q + 4, :].bitcast(I32),
                    in_=picked_s[16 * a + 4 * q : 16 * a + 4 * q + 4, :].bitcast(I32),
                )

        def entries(listed, first, last):
            return listed[:, first // PER_COLUMN : last // PER_COLUMN]

        v_w = {}
        for u in range(HALVES):
            for a in range(PASSES):
                v_w[a, u] = held([P, BANK], U32, "v_w%d%d" % (a, u))
                window = tab_w[a][:].bitcast(U32)
                nc.vector.tensor_copy(v_w[a, u][:], window.indirect(entries(pick, u * BANK, (u + 1) * BANK)))

        def mx_bank():
            return psum.tile([P, BANK], F32, name="bank", tag="mx", bufs=MX_BANKS)

        def product(u, codes, scales):
            banks = [mx_bank() for b in range(BLOCKS)]
            for a in range(PASSES):
                for b in range(BLOCKS):
                    nc.tensor.matmul_mx(
                        out=banks[b][:],
                        lhsT=v_w[a, u][:, b * P : (b + 1) * P].bitcast(E4M3),
                        lhsT_scale=v_s[a][:, u * BANK + b * P : u * BANK + (b + 1) * P],
                        rhs=codes[a],
                        rhs_scale=scales[a],
                        start=(a == 0),
                        stop=(a == PASSES - 1),
                    )
            return banks

        def dealt(bank):
            return bank[:].rearrange("j (m t) -> j t m", t=PACK)

        def by_tile(tile):
            return tile[:].rearrange("j (t m) -> j t m", t=PACK)

        w1_c = []
        w1_s = []

        def quantise_w1(a):
            woven = ring.tile([P, H, PACK], BF16, name="woven", tag="woven", align_bytes=64)
            nc.vector.tensor_copy(
                woven[:].rearrange("p (c e) i -> p c i e", e=LINE),
                w1_raw[a][:].rearrange("p i (c e) -> p c i e", e=LINE),
            )
            w1_c.append(held([P, H], U32, "w1_c%d" % a))
            w1_s.append(held([P, H], U8, "w1_s%d" % a))
            nc.vector.quantize_mx(out=w1_c[a][:].bitcast(E4M3), scales=w1_s[a][:], in_=woven[:].rearrange("p n i -> p (n i)"))

        term_tags = [["term%d" % b for b in range(BLOCKS)], ["gain10", "fresh10", "gain20", "fresh20"]]

        for u in range(HALVES):
            bent = [staged("bent", BANK) for b in range(BLOCKS)]
            third = [staged("third", BANK) for b in range(BLOCKS)]
            banks = product(u, [w2_w[:, a, :].bitcast(E2M1) for a in range(PASSES)], [w2_s[:, a, :] for a in range(PASSES)])
            for b in range(BLOCKS):
                nc.scalar.activation(by_tile(bent[b]), dealt(banks[b]), ACT.Tanh)
            banks = product(u, [w3_w[:, a, :].bitcast(E4M3) for a in range(PASSES)], [w3_s[:, a, :] for a in range(PASSES)])
            for b in range(BLOCKS):
                nc.scalar.copy(by_tile(third[b]), dealt(banks[b]))
            if u == 0:
                for a in range(PASSES):
                    quantise_w1(a)
            banks = product(u, [w1_c[a][:].bitcast(E4M3) for a in range(PASSES)], [w1_s[a][:] for a in range(PASSES)])
            term = []
            for b in range(BLOCKS):
                term.append(keep.tile([P, BANK], F32, name="term", tag=term_tags[u][b]))
                nc.vector.tensor_tensor(by_tile(term[b]), dealt(banks[b]), by_tile(bent[b]), ALU.mult)
            for t in range(PACK):
                rows = slice(t * P, (t + 1) * P)
                fresh = keep.tile([P, BANK], F32, name="fresh", tag="fresh%d%d" % (t, u))
                step = BLOCKS // 2 if (t, u) == (0, 0) else BLOCKS
                for b0 in range(0, BLOCKS, step):
                    turned = psum.tile([P, step * P], F32, name="turned", tag="turned", bufs=TURN_BANKS)
                    for b in range(step):
                        cols = slice(b * P, (b + 1) * P)
                        nc.tensor.matmul(turned[:, cols], lhsT=third[b0 + b][:, rows], rhs=ident[:], is_transpose=True, start=True, stop=False)
                        nc.tensor.matmul(turned[:, cols], lhsT=term[b0 + b][:, rows], rhs=ident[:], is_transpose=True, start=False, stop=True)
                    part = slice(b0 * P, (b0 + step) * P)
                    nc.scalar.copy(fresh[:, part], turned[:])
                    places = entries(put, u * BANK + part.start, u * BANK + part.stop)
                    nc.vector.tensor_tensor(page[t][:].indirect(places), fresh[:, part], gain[t, u][:, part], ALU.mult)

        w4_raw = load_rows(w4)
        skip_t = held([P, PACK], F32, "skip_t")
        nc.sync.dma_start(out=skip_t[:], in_=skip.rearrange("(p t) -> p t", t=PACK))
        w4_woven = ring.tile([P, H, PACK], BF16, name="w4_woven", tag="woven", align_bytes=64)
        nc.scalar.copy(
            w4_woven[:].rearrange("p (t m) i -> p t m i", t=PACK),
            w4_raw[:].rearrange("p i (m t) -> p t m i", t=PACK),
        )
        w4_c = held([P, H], U32, "w4_c")
        w4_s = held([P, H], U8, "w4_s")

        rounded = [held([P, last - first, PACK], BF16, "rounded%d" % first) for first, last in SPANS]

        for t in range(PACK):
            kept = ring.tile([P, PAIRS], F32, name="kept")
            swapped = ring.tile([P, PAIRS], F32, name="swapped")
            high = ring.tile([P, PAIRS], F32, name="high")
            low = ring.tile([P, PAIRS], F32, name="low")
            nc.vector.tensor_copy(kept[:], page[t][:].indirect(larger[:]))
            nc.vector.tensor_copy(swapped[:], page[t][:].indirect(smaller[:]))
            if t + 1 == PACK:
                nc.vector.quantize_mx(out=w4_c[:].bitcast(E4M3), scales=w4_s[:], in_=w4_woven[:].rearrange("p n i -> p (n i)"))
            nc.vector.tensor_tensor(high[:], kept[:], swapped[:], ALU.max)
            nc.vector.tensor_tensor(low[:], kept[:], swapped[:], ALU.min)
            nc.vector.tensor_copy(page[t][:].indirect(larger[:]), high[:])
            nc.vector.tensor_copy(page[t][:].indirect(smaller[:]), low[:])
            for c, (first, last) in enumerate(SPANS):
                nc.scalar.copy(rounded[c][:, :, t], page[t][:, first:last])

        out_rows = out.rearrange("(p t) c -> p t c", t=PACK)
        for c, (first, last) in enumerate(SPANS):
            width = last - first
            page_c = held([P, width], U32, "page_c%d" % c)
            page_s = held([P, width], U8, "page_s%d" % c)
            nc.vector.quantize_mx(out=page_c[:].bitcast(E4M3), scales=page_s[:], in_=rounded[c][:].rearrange("p n i -> p (n i)"))
            for t in range(PACK):
                rows = slice(t * P, (t + 1) * P)
                bank = mx_bank()
                nc.tensor.matmul_mx(
                    out=bank[:, 0:width], lhsT=w4_c[:, rows].bitcast(E4M3), lhsT_scale=w4_s[:, rows],
                    rhs=page_c[:].bitcast(E4M3), rhs_scale=page_s[:], start=True, stop=True,
                )
                result = staged("result", width)
                nc.vector.scalar_tensor_tensor(result[:], page[t][:, first:last], skip_t[:, t : t + 1], bank[:, 0:width], ALU.mult, ALU.add)
                nc.sync.dma_start(out=out_rows[:, t, first:last], in_=result[:])
